import numpy as np
import ml_dtypes


def mxq(x, axis, fmt="e4m3"):
    dtype, down = {"e4m3": (ml_dtypes.float8_e4m3fn, 7), "e5m2": (ml_dtypes.float8_e5m2, 14)}[fmt]
    v = np.moveaxis(np.asarray(x, np.float32).astype(ml_dtypes.bfloat16).astype(np.float64), axis, -1)
    blocks = v.reshape(v.shape[:-1] + (-1, 32))
    amax = np.abs(blocks).max(-1, keepdims=True)
    byte = np.maximum(np.where(amax > 0, np.frexp(amax)[1] - 1 + 127, 0) - down, 1)
    scale = np.exp2(byte - 127.0)
    codes = (blocks / scale).astype(np.float32).astype(dtype).astype(np.float64)
    return np.moveaxis((codes * scale).reshape(v.shape), -1, axis)


WIDE = False


def mx_kscale(k):
    if not WIDE:
        return np.ones(k)
    levels = np.array([10, -10, 5, -5, 0])
    if k % 512:
        return np.exp2(np.random.permutation(np.resize(levels, k // 32))).repeat(32)
    a = np.empty((k // 512, 16))
    for p in range(k // 512):
        a[p, :8] = np.random.permutation(np.resize(levels, 8))
        for g in range(8):
            far = levels[np.abs(levels - a[p, g]) >= 10]
            a[p, g + 8] = far[np.random.randint(len(far))]
    return np.exp2(a.ravel()).repeat(32)


BF16 = ml_dtypes.bfloat16


def bf(x):
    return np.asarray(x, np.float32).astype(BF16)


def f64(x):
    return np.asarray(x).astype(np.float64)


T, P, Q, R = 256, 8, 64, 8
PQ = P * Q
QR = Q * R


def apply_pq(x, t1):
    n_t, n_p, n_q, n_r = x.shape
    xa = np.transpose(x, (0, 3, 1, 2)).reshape(n_t * n_r, n_p * n_q)
    h = mxq(xa, 1, "e4m3") @ mxq(t1, 0, "e4m3")
    return h.reshape(n_t, n_r, n_p, n_q)


def apply_qr(h, t2):
    n_t, n_r, n_p, n_q = h.shape
    hb = np.transpose(h, (0, 2, 3, 1)).reshape(n_t * n_p, n_q * n_r)
    z = mxq(hb, 1, "e4m3") @ mxq(t2, 0, "e4m3")
    return z.reshape(n_t, n_p, n_q, n_r)


def draw0():
    a = mx_kscale(PQ)
    g = mx_kscale(QR).reshape(Q, R)[:, 0]
    return {
        "x": bf(np.random.standard_normal((T, P, Q, R)) * a.reshape(P, Q)[None, :, :, None]),
        "t1": bf(np.random.standard_normal((PQ, PQ)) / np.sqrt(PQ) / a[:, None] * np.tile(g, P)[None, :]),
        "t2": bf(np.random.standard_normal((QR, QR)) / np.sqrt(QR) / np.repeat(g, R)[:, None]),
        "s": bf(1.0 + 0.1 * np.random.standard_normal((P, Q, R))),
        "y0": bf(np.random.standard_normal((T, P, Q, R))),
    }


def core(x, t1, t2, s, y0):
    h = apply_pq(f64(x), f64(t1))
    z = apply_qr(h, f64(t2))
    return f64(y0) + f64(s)[None, :, :, :] * z


def e4m3fn_bytes(y):
    return np.clip(np.asarray(y, np.float64), -448.0, 448.0).astype(np.float32).astype(ml_dtypes.float8_e4m3fn).view(np.uint8)


def e4m3fn_values(b):
    return np.asarray(b, np.uint8).view(ml_dtypes.float8_e4m3fn).astype(np.float64)


def setup_inputs():
    d = draw0()
    x0 = np.asarray(d['t2']).astype(np.float64)
    s = (np.max(np.abs(x0), axis=(1,), keepdims=True) / 448.0).astype(np.float32)
    out = {}
    for k, v in d.items():
        if k == 't2':
            out['t2_bytes'] = e4m3fn_bytes(x0 / s.astype(np.float64))
            out['t2_scale'] = s
        else:
            out[k] = v
    return out


def reference(x, t1, t2_bytes, t2_scale, s, y0):
    return core(x, t1, e4m3fn_values(t2_bytes) * t2_scale.astype(np.float64), s, y0)

@@ -1,0 +1,226 @@
+from contextlib import ExitStack
+
+import concourse.mybir as mybir
+from concourse.masks import make_identity
+
+T, K = 256, 512
+FLOPS = 2 * 2 * (T * 8) * K * K
+
+F32 = mybir.dt.float32
+BF16 = mybir.dt.bfloat16
+I32 = mybir.dt.int32
+U32 = mybir.dt.uint32
+U8 = mybir.dt.uint8
+FP8 = mybir.dt.float8_e4m3fn
+FP8X4 = mybir.dt.float8_e4m3fn_x4
+MULT = mybir.AluOpType.mult
+ADD = mybir.AluOpType.add
+
+P = 128
+UNITS = 16
+LEAD = 3
+
+
+def tile_quantatwoaxispairtensorupdate_kernel(tc, x, t1, t2_bytes, t2_scale, s, y0, out):
+    nc = tc.nc
+    x_rows = x.rearrange("t p q r -> t (p q r)")
+    y_rows = y0.rearrange("t (h a) c d -> (t h) (a c d)", h=2)
+    o_rows = out.rearrange("t (h a) c d -> (t h) (a c d)", h=2)
+    s_rows = s.rearrange("(h a) c d -> h (a c d)", h=2)
+
+    with ExitStack() as ctx:
+        sb = ctx.enter_context(tc.tile_pool(name="sb", bufs=1))
+        ps = ctx.enter_context(tc.psum_pool(name="ps", bufs=1))
+        ctx.enter_context(tc.manual_schedule())
+
+        def tiles(name, n, shape, dtype):
+            return [sb.tile(shape, dtype, name="%s%d" % (name, i), align_bytes=256) for i in range(n)]
+
+        banks = [ps.tile([P, 512], F32, name="bank%d" % i) for i in range(8)]
+        t_banks = banks[0:2]
+        h_banks = banks[2:5]
+        z_banks = banks[5:8]
+
+        ident = sb.tile([P, P], F32, align_bytes=256)
+        t2_raw = sb.tile([P, 4, K], U8, align_bytes=256)
+        t2_sc = sb.tile([P, 4], F32, align_bytes=256)
+        t2_wide = sb.tile([P, 4, K], BF16, align_bytes=256)
+        t2_grp = sb.tile([P, K, 4], BF16, align_bytes=256)
+        t2_codes = sb.tile([P, K], U32, align_bytes=256)
+        t2_plane = sb.tile([P, K], U8, align_bytes=256)
+        t1_raw = sb.tile([P, 4, K], BF16, align_bytes=256)
+        t1_grp = sb.tile([P, K, 4], BF16, align_bytes=256)
+        t1_codes = sb.tile([P, 3, K], U32, align_bytes=256)
+        t1_plane = sb.tile([P, K], U8, align_bytes=256)
+        w_codes = tiles("w_codes", 2, [P, K, 2], U32)
+        w_plane = sb.tile([P, K, 2], U8, align_bytes=256)
+        s_sb = sb.tile([P, 4 * K], BF16, align_bytes=256)
+        x_sb = tiles("x_sb", 2, [P, 8 * K], BF16)
+        y_sb = tiles("y_sb", 4, [P, 4 * K], BF16)
+        x_grp = tiles("x_grp", 4, [P, 2048], BF16)
+        x_codes = tiles("x_codes", 4, [P, 512], U32)
+        x_plane = tiles("x_plane", 4, [P, 512], U8)
+        h_grp = tiles("h_grp", UNITS // 2, [P, 1024], BF16)
+        h_codes = tiles("h_codes", UNITS // 2, [P, 2 * P], U32)
+        h_plane = tiles("h_plane", UNITS // 2, [P, 2 * P], U8)
+        sz = tiles("sz", UNITS // 2, [P, 2 * K], F32)
+        res = tiles("res", UNITS // 2, [P, 2 * K], F32)
+
+        nc.sync.dma_start(out=t2_raw[:], in_=t2_bytes.rearrange("(p j) n -> p j n", j=4))
+        nc.sync.dma_start(out=t2_sc[:], in_=t2_scale.rearrange("(p j) o -> p (j o)", j=4))
+        nc.sync.dma_start(out=x_sb[0][:], in_=x_rows[0:P, :])
+        nc.sync.dma_start(out=t1_raw[:], in_=t1.rearrange("(p j) n -> p j n", j=4))
+        nc.sync.dma_start(out=x_sb[1][:], in_=x_rows[P : 2 * P, :])
+        nc.sync.dma_start(out=s_sb[:], in_=s_rows.partition_broadcast(64))
+        for g in range(4):
+            nc.sync.dma_start(out=y_sb[g][:], in_=y_rows[g * P : (g + 1) * P, :])
+
+        make_identity(nc, ident[:])
+        nc.gpsimd.memset(t1_codes[:, 0, :], 0)
+        nc.gpsimd.memset(t1_codes[:, 2, :], 0)
+        nc.gpsimd.memset(t1_plane[:].bitcast(U32), 0)
+
+        def interleave(grp, raw):
+            nc.vector.tensor_copy(
+                out=grp[:].rearrange("p (c i) j -> p c j i", i=4),
+                in_=raw[:].rearrange("p j (c i) -> p c j i", i=4),
+            )
+
+        def turn_x(tt, rr, bank):
+            words = x_sb[tt][:].bitcast(F32)
+            for j in range(4):
+                nc.tensor.transpose(bank[:, j * P : (j + 1) * P], words[:, 4 * j + rr : 2048 : 16], ident[:])
+
+        def copy_x(tt, rr, bank):
+            dst = x_grp[2 * tt + rr // 2][:].rearrange("p (t q e j) -> p t q e j", q=2, e=2, j=4)
+            nc.scalar.copy(
+                out=dst[:, :, rr % 2, :, :],
+                in_=bank[:].bitcast(BF16).rearrange("p (j t e) -> p t e j", j=4, e=2),
+            )
+
+        def quant_x(tt, rh, lo, hi):
+            n = 2 * tt + rh
+            nc.vector.quantize_mx(
+                out=x_codes[n][:, lo * 256 : hi * 256].bitcast(FP8X4),
+                scales=x_plane[n][:, lo * 256 : hi * 256],
+                in_=x_grp[n][:, lo * 1024 : hi * 1024],
+            )
+
+        def first_product(u):
+            g, ap = divmod(u, 4)
+            bank = h_banks[u % 3]
+            cols = slice((g % 2) * 256, (g % 2 + 1) * 256)
+            for hi in range(2):
+                a = 4 * hi + ap
+                for rh in range(2):
+                    nc.tensor.matmul_mx(
+                        out=bank[:, hi * 256 : (hi + 1) * 256],
+                        lhsT=w_codes[rh][:].rearrange("p c z -> p (c z)")[:, a * P : (a + 1) * P].bitcast(FP8X4),
+                        lhsT_scale=w_plane[:].rearrange("p c z -> p (c z)")[:, a * P : (a + 1) * P],
+                        rhs=x_codes[2 * (g // 2) + rh][:, cols].bitcast(FP8X4),
+                        rhs_scale=x_plane[2 * (g // 2) + rh][:, cols],
+                        start=(rh == 0),
+                        stop=(rh == 1),
+                    )
+            nc.scalar.copy(
+                out=h_grp[u // 2][:, (u % 2) * K : (u % 2 + 1) * K].rearrange("p (t h r) -> p t h r", h=2, r=4),
+                in_=bank[:].rearrange("p (h t r) -> p t h r", h=2, r=4),
+            )
+
+        def quant_h(u, n):
+            lo, hi = u % 2, u % 2 + n
+            nc.vector.quantize_mx(
+                out=h_codes[u // 2][:, lo * P : hi * P].bitcast(FP8X4),
+                scales=h_plane[u // 2][:, lo * P : hi * P],
+                in_=h_grp[u // 2][:, lo * K : hi * K],
+            )
+
+        def second_product(u):
+            cols = slice((u % 2) * P, (u % 2 + 1) * P)
+            nc.tensor.matmul_mx(
+                out=z_banks[u % 3][:],
+                lhsT=h_codes[u // 2][:, cols].bitcast(FP8X4),
+                lhsT_scale=h_plane[u // 2][:, cols],
+                rhs=t2_codes[:].bitcast(FP8X4),
+                rhs_scale=t2_plane[:],
+                start=True,
+                stop=True,
+            )
+
+        def scale_z(u):
+            ap = u % 4
+            nc.vector.tensor_tensor(
+                out=sz[u // 2][:, (u % 2) * K : (u % 2 + 1) * K],
+                in0=z_banks[u % 3][:],
+                in1=s_sb[:, ap * K : (ap + 1) * K],
+                op=MULT,
+            )
+
+        def add_store(u, n):
+            g, ap = divmod(u, 4)
+            own = slice((u % 2) * K, (u % 2 + n) * K)
+            cols = slice(ap * K, (ap + n) * K)
+            nc.vector.tensor_tensor(out=res[u // 2][:, own], in0=sz[u // 2][:, own], in1=y_sb[g][:, cols], op=ADD)
+            nc.sync.dma_start(out=o_rows[g * P : (g + 1) * P, cols], in_=res[u // 2][:, own])
+
+        for j in range(4):
+            nc.vector.tensor_scalar(
+                out=t2_wide[:, j, :],
+                in0=t2_raw[:, j, :].bitcast(FP8),
+                scalar1=t2_sc[:, j : j + 1],
+                scalar2=None,
+                op0=MULT,
+            )
+        interleave(t2_grp, t2_wide)
+        nc.vector.quantize_mx(
+            out=t2_codes[:].bitcast(FP8X4), scales=t2_plane[:], in_=t2_grp[:].rearrange("p c j -> p (c j)")
+        )
+
+        head_banks = [banks[0], banks[1], banks[6], banks[7]]
+        for rr in range(4):
+            turn_x(0, rr, head_banks[rr])
+            copy_x(0, rr, head_banks[rr])
+
+        interleave(t1_grp, t1_raw)
+        nc.vector.quantize_mx(
+            out=t1_codes[:, 1, :].bitcast(FP8X4), scales=t1_plane[:], in_=t1_grp[:].rearrange("p c j -> p (c j)")
+        )
+        quant_x(0, 0, 0, 1)
+        for rh in range(2):
+            nc.vector.tensor_copy(
+                out=w_codes[rh][:].bitcast(I32),
+                in_=t1_codes[:, 1 - rh : 3 - rh, :].bitcast(I32).rearrange("p z c -> p c z"),
+            )
+            nc.vector.tensor_copy(out=w_plane[:, :, rh], in_=t1_plane[:])
+        quant_x(0, 1, 0, 1)
+        turn_x(1, 0, t_banks[0])
+
+        first_product(0)
+        first_product(1)
+        quant_x(0, 0, 1, 2)
+        quant_h(0, 1)
+        second_product(0)
+        first_product(2)
+        for step in range(1, UNITS + 1):
+            if step == 1:
+                copy_x(1, 0, t_banks[0])
+                quant_h(1, 1)
+            if step < 4:
+                turn_x(1, step, t_banks[step % 2])
+            if step + LEAD - 1 < UNITS:
+                first_product(step + LEAD - 1)
+            if step % 2 == 0 and step < UNITS:
+                quant_h(step, 2)
+            if step < UNITS:
+                second_product(step)
+            if step == 1:
+                quant_x(0, 1, 1, 2)
+            if step < 4:
+                copy_x(1, step, t_banks[step % 2])
+            scale_z(step - 1)
+            if step in (3, 5):
+                quant_x(1, (step - 3) // 2, 0, 2)
+            if step % 2 == 1 and step >= 3:
+                add_store(step - 3, 2)
+        add_store(UNITS - 2, 1)
+        add_store(UNITS - 1, 1)

@@ -15,10 +15,16 @@ FP8 = mybir.dt.float8_e4m3fn
 FP8X4 = mybir.dt.float8_e4m3fn_x4
 MULT = mybir.AluOpType.mult
 ADD = mybir.AluOpType.add
+COPY = mybir.ActivationFunctionType.Copy
 
 P = 128
-UNITS = 16
-LEAD = 3
+UNITS = 12
+TURNED = (2, 6, 3, 7)
+
+
+def place(u):
+    pair = u // 2
+    return 2 * (pair // 4) + pair % 2, 2 * (pair // 2 % 2) + u % 2
 
 
 def tile_quantatwoaxispairtensorupdate_kernel(tc, x, t1, t2_bytes, t2_scale, s, y0, out):
@@ -26,6 +32,8 @@ def tile_quantatwoaxispairtensorupdate_kernel(tc, x, t1, t2_bytes, t2_scale, s, 
     x_rows = x.rearrange("t p q r -> t (p q r)")
     y_rows = y0.rearrange("t (h a) c d -> (t h) (a c d)", h=2)
     o_rows = out.rearrange("t (h a) c d -> (t h) (a c d)", h=2)
+    y_tok = y0.rearrange("t (h a) c d -> t h (a c d)", h=2)
+    o_tok = out.rearrange("t a c d -> t a (c d)")
     s_rows = s.rearrange("(h a) c d -> h (a c d)", h=2)
 
     with ExitStack() as ctx:
@@ -37,9 +45,13 @@ def tile_quantatwoaxispairtensorupdate_kernel(tc, x, t1, t2_bytes, t2_scale, s, 
             return [sb.tile(shape, dtype, name="%s%d" % (name, i), align_bytes=256) for i in range(n)]
 
         banks = [ps.tile([P, 512], F32, name="bank%d" % i) for i in range(8)]
-        t_banks = banks[0:2]
-        h_banks = banks[2:5]
-        z_banks = banks[5:8]
+
+        def h_bank(u):
+            return banks[4 + u % 4] if u < 8 else banks[4 + u % 2]
+
+        def z_bank(u):
+            return banks[2 + u % 2]
+
 
         ident = sb.tile([P, P], F32, align_bytes=256)
         t2_raw = sb.tile([P, 4, K], U8, align_bytes=256)
@@ -49,14 +61,24 @@ def tile_quantatwoaxispairtensorupdate_kernel(tc, x, t1, t2_bytes, t2_scale, s, 
         t2_codes = sb.tile([P, K], U32, align_bytes=256)
         t2_plane = sb.tile([P, K], U8, align_bytes=256)
         t1_raw = sb.tile([P, 4, K], BF16, align_bytes=256)
-        t1_grp = sb.tile([P, K, 4], BF16, align_bytes=256)
-        t1_codes = sb.tile([P, 3, K], U32, align_bytes=256)
-        t1_plane = sb.tile([P, K], U8, align_bytes=256)
-        w_codes = tiles("w_codes", 2, [P, K, 2], U32)
-        w_plane = sb.tile([P, K, 2], U8, align_bytes=256)
+        t1_grp = tiles("t1_grp", 2, [P, 256, 4], BF16)
+        t1_codes = tiles("t1_codes", 2, [P, 3, 256], U32)
+        t1_plane = tiles("t1_plane", 2, [P, 256], U8)
+        w_codes = tiles("w_codes", 4, [P, 256, 2], U32)
+        w_plane = tiles("w_plane", 2, [P, 256, 2], U8)
         s_sb = sb.tile([P, 4 * K], BF16, align_bytes=256)
-        x_sb = tiles("x_sb", 2, [P, 8 * K], BF16)
-        y_sb = tiles("y_sb", 4, [P, 4 * K], BF16)
+        x_part = tiles("x_part", 4, [P, 1024], BF16)
+        x_late = tiles("x_late", 2, [P, 2048], BF16)
+        x_perm = tiles("x_perm", 2, [P, 16, P], F32)
+        y_sb = tiles("y_sb", 2, [P, 4 * K], BF16) + tiles("y_half", 2, [P, 2 * K], BF16)
+        y_turn = sb.tile([P, 2, 2 * K], BF16, align_bytes=256)
+        ident_bf = sb.tile([P, P], BF16, align_bytes=256)
+        s_col = sb.tile([P, 16], F32, align_bytes=256)
+        r_grp = tiles("r_grp", 2, [P, 1024], BF16)
+        r_codes = tiles("r_codes", 2, [P, 2 * P], U32)
+        r_plane = tiles("r_plane", 2, [P, 2 * P], U8)
+        r_sz = tiles("r_sz", 4, [P, K], F32)
+        r_res = tiles("r_res", 4, [P, K], F32)
         x_grp = tiles("x_grp", 4, [P, 2048], BF16)
         x_codes = tiles("x_codes", 4, [P, 512], U32)
         x_plane = tiles("x_plane", 4, [P, 512], U8)
@@ -68,17 +90,22 @@ def tile_quantatwoaxispairtensorupdate_kernel(tc, x, t1, t2_bytes, t2_scale, s, 
 
         nc.sync.dma_start(out=t2_raw[:], in_=t2_bytes.rearrange("(p j) n -> p j n", j=4))
         nc.sync.dma_start(out=t2_sc[:], in_=t2_scale.rearrange("(p j) o -> p (j o)", j=4))
-        nc.sync.dma_start(out=x_sb[0][:], in_=x_rows[0:P, :])
+        for c in range(4):
+            nc.sync.dma_start(out=x_part[c][:], in_=x_rows[0:P, c * 1024 : (c + 1) * 1024])
         nc.sync.dma_start(out=t1_raw[:], in_=t1.rearrange("(p j) n -> p j n", j=4))
-        nc.sync.dma_start(out=x_sb[1][:], in_=x_rows[P : 2 * P, :])
+        for c in range(2):
+            nc.sync.dma_start(out=x_late[c][:], in_=x_rows[P : 2 * P, c * 2048 : (c + 1) * 2048])
         nc.sync.dma_start(out=s_sb[:], in_=s_rows.partition_broadcast(64))
         for g in range(4):
-            nc.sync.dma_start(out=y_sb[g][:], in_=y_rows[g * P : (g + 1) * P, :])
+            nc.sync.dma_start(out=y_sb[g][:], in_=y_rows[g * P : (g + 1) * P, 0 : (4 * K if g < 2 else 2 * K)])
+        nc.sync.dma_start(out=y_turn[:], in_=y_tok[P : 2 * P, :, 2 * K : 4 * K])
 
         make_identity(nc, ident[:])
-        nc.gpsimd.memset(t1_codes[:, 0, :], 0)
-        nc.gpsimd.memset(t1_codes[:, 2, :], 0)
-        nc.gpsimd.memset(t1_plane[:].bitcast(U32), 0)
+        make_identity(nc, ident_bf[:])
+        for half in range(2):
+            nc.gpsimd.memset(t1_codes[half][:, 0, :], 0)
+            nc.gpsimd.memset(t1_codes[half][:, 2, :], 0)
+            nc.gpsimd.memset(t1_plane[half][:].bitcast(U32), 0)
 
         def interleave(grp, raw):
             nc.vector.tensor_copy(
@@ -86,17 +113,51 @@ def tile_quantatwoaxispairtensorupdate_kernel(tc, x, t1, t2_bytes, t2_scale, s, 
                 in_=raw[:].rearrange("p j (c i) -> p c j i", i=4),
             )
 
-        def turn_x(tt, rr, bank):
-            words = x_sb[tt][:].bitcast(F32)
-            for j in range(4):
-                nc.tensor.transpose(bank[:, j * P : (j + 1) * P], words[:, 4 * j + rr : 2048 : 16], ident[:])
+        def order_x(c):
+            nc.scalar.copy(
+                out=x_perm[0][:, :, c * 32 : (c + 1) * 32].rearrange("p (j r) (g l) -> p j g r l", j=4, l=4),
+                in_=x_part[c][:].bitcast(F32).rearrange("p (g l j r) -> p j g r l", l=4, j=4, r=4),
+            )
 
-        def copy_x(tt, rr, bank):
+        def order_late_x(c):
+            nc.vector.tensor_copy(
+                out=x_perm[1][:, :, c * 64 : (c + 1) * 64].rearrange("p (j r) (g l) -> p j g r l", j=4, l=4),
+                in_=x_late[c][:].bitcast(F32).rearrange("p (g l j r) -> p j g r l", l=4, j=4, r=4),
+            )
+
+        def turn_x(tt, rr, bank):
+            for j in range(4):
+                nc.tensor.transpose(bank[:, j * P : (j + 1) * P], x_perm[tt][:, 4 * j + rr, :], ident[:])
+
+        def copy_x(tt, rr, bank, lo, hi):
             dst = x_grp[2 * tt + rr // 2][:].rearrange("p (t q e j) -> p t q e j", q=2, e=2, j=4)
             nc.scalar.copy(
-                out=dst[:, :, rr % 2, :, :],
-                in_=bank[:].bitcast(BF16).rearrange("p (j t e) -> p t e j", j=4, e=2),
+                out=dst[:, lo * 64 : hi * 64, rr % 2, :, :],
+                in_=bank[:].bitcast(BF16).rearrange("p (j t e) -> p t e j", j=4, e=2)[:, lo * 64 : hi * 64, :, :],
             )
+
+        def group_t1(half):
+            nc.vector.tensor_copy(
+                out=t1_grp[half][:].rearrange("p (h c i) j -> p h c j i", h=2, i=4),
+                in_=t1_raw[:].rearrange("p j (h f c i) -> p f h c j i", h=2, f=2, i=4)[:, half],
+            )
+
+        def quant_t1(half):
+            nc.vector.quantize_mx(
+                out=t1_codes[half][:, 1, :].bitcast(FP8X4),
+                scales=t1_plane[half][:],
+                in_=t1_grp[half][:].rearrange("p c j -> p (c j)"),
+            )
+
+        def spread_t1(half, rh):
+            nc.vector.tensor_copy(
+                out=w_codes[2 * half + rh][:].bitcast(I32),
+                in_=t1_codes[half][:, 1 - rh : 3 - rh, :].bitcast(I32).rearrange("p z c -> p c z"),
+            )
+
+        def spread_t1_scales(half):
+            for z in range(2):
+                nc.vector.tensor_copy(out=w_plane[half][:, :, z], in_=t1_plane[half][:])
 
         def quant_x(tt, rh, lo, hi):
             n = 2 * tt + rh
@@ -106,26 +167,31 @@ def tile_quantatwoaxispairtensorupdate_kernel(tc, x, t1, t2_bytes, t2_scale, s, 
                 in_=x_grp[n][:, lo * 1024 : hi * 1024],
             )
 
-        def first_product(u):
-            g, ap = divmod(u, 4)
-            bank = h_banks[u % 3]
+        def first_pass(u, rh):
+            g, ap = place(u)
             cols = slice((g % 2) * 256, (g % 2 + 1) * 256)
             for hi in range(2):
-                a = 4 * hi + ap
-                for rh in range(2):
-                    nc.tensor.matmul_mx(
-                        out=bank[:, hi * 256 : (hi + 1) * 256],
-                        lhsT=w_codes[rh][:].rearrange("p c z -> p (c z)")[:, a * P : (a + 1) * P].bitcast(FP8X4),
-                        lhsT_scale=w_plane[:].rearrange("p c z -> p (c z)")[:, a * P : (a + 1) * P],
-                        rhs=x_codes[2 * (g // 2) + rh][:, cols].bitcast(FP8X4),
-                        rhs_scale=x_plane[2 * (g // 2) + rh][:, cols],
-                        start=(rh == 0),
-                        stop=(rh == 1),
-                    )
+                own = slice((2 * hi + ap % 2) * P, (2 * hi + ap % 2 + 1) * P)
+                nc.tensor.matmul_mx(
+                    out=h_bank(u)[:, hi * 256 : (hi + 1) * 256],
+                    lhsT=w_codes[2 * (ap // 2) + rh][:].rearrange("p c z -> p (c z)")[:, own].bitcast(FP8X4),
+                    lhsT_scale=w_plane[ap // 2][:].rearrange("p c z -> p (c z)")[:, own],
+                    rhs=x_codes[2 * (g // 2) + rh][:, cols].bitcast(FP8X4),
+                    rhs_scale=x_plane[2 * (g // 2) + rh][:, cols],
+                    start=(rh == 0 and hi == 0),
+                    stop=(rh == 1 and hi == 1),
+                )
+
+        def copy_h(u):
             nc.scalar.copy(
                 out=h_grp[u // 2][:, (u % 2) * K : (u % 2 + 1) * K].rearrange("p (t h r) -> p t h r", h=2, r=4),
-                in_=bank[:].rearrange("p (h t r) -> p t h r", h=2, r=4),
+                in_=h_bank(u)[:].rearrange("p (h t r) -> p t h r", h=2, r=4),
             )
+
+        def first_product(u):
+            first_pass(u, 0)
+            first_pass(u, 1)
+            copy_h(u)
 
         def quant_h(u, n):
             lo, hi = u % 2, u % 2 + n
@@ -138,7 +204,7 @@ def tile_quantatwoaxispairtensorupdate_kernel(tc, x, t1, t2_bytes, t2_scale, s, 
         def second_product(u):
             cols = slice((u % 2) * P, (u % 2 + 1) * P)
             nc.tensor.matmul_mx(
-                out=z_banks[u % 3][:],
+                out=z_bank(u)[:],
                 lhsT=h_codes[u // 2][:, cols].bitcast(FP8X4),
                 lhsT_scale=h_plane[u // 2][:, cols],
                 rhs=t2_codes[:].bitcast(FP8X4),
@@ -148,20 +214,96 @@ def tile_quantatwoaxispairtensorupdate_kernel(tc, x, t1, t2_bytes, t2_scale, s, 
             )
 
         def scale_z(u):
-            ap = u % 4
+            ap = place(u)[1]
             nc.vector.tensor_tensor(
                 out=sz[u // 2][:, (u % 2) * K : (u % 2 + 1) * K],
-                in0=z_banks[u % 3][:],
+                in0=z_bank(u)[:],
                 in1=s_sb[:, ap * K : (ap + 1) * K],
                 op=MULT,
             )
 
         def add_store(u, n):
-            g, ap = divmod(u, 4)
+            g, ap = place(u)
             own = slice((u % 2) * K, (u % 2 + n) * K)
             cols = slice(ap * K, (ap + n) * K)
             nc.vector.tensor_tensor(out=res[u // 2][:, own], in0=sz[u // 2][:, own], in1=y_sb[g][:, cols], op=ADD)
             nc.sync.dma_start(out=o_rows[g * P : (g + 1) * P, cols], in_=res[u // 2][:, own])
+
+        def turn_s(bank):
+            for n in range(8):
+                nc.tensor.matmul(
+                    out=bank[:, 2 * n : 2 * n + 2],
+                    lhsT=s_sb[:, 2 * K + n * P : 2 * K + (n + 1) * P],
+                    rhs=ident_bf[:, 0:2],
+                    start=True,
+                    stop=True,
+                )
+            nc.scalar.copy(out=s_col[:], in_=bank[:, 0:16])
+
+        def turned_first(n):
+            hi, ap = divmod(TURNED[n], 4)
+            own = slice((2 * hi + ap % 2) * P, (2 * hi + ap % 2 + 1) * P)
+            bank = banks[6 + n % 2]
+            for rh in range(2):
+                nc.tensor.matmul_mx(
+                    out=bank[:],
+                    lhsT=w_codes[2 + rh][:].rearrange("p c z -> p (c z)")[:, own].bitcast(FP8X4),
+                    lhsT_scale=w_plane[1][:].rearrange("p c z -> p (c z)")[:, own],
+                    rhs=x_codes[2 + rh][:].bitcast(FP8X4),
+                    rhs_scale=x_plane[2 + rh][:],
+                    start=(rh == 0),
+                    stop=(rh == 1),
+                )
+            nc.scalar.copy(out=r_grp[n // 2][:, (n % 2) * K : (n % 2 + 1) * K], in_=bank[:])
+
+        def turned_quant(m):
+            nc.vector.quantize_mx(out=r_codes[m][:].bitcast(FP8X4), scales=r_plane[m][:], in_=r_grp[m][:])
+
+        def turned_second(n):
+            cols = slice((n % 2) * P, (n % 2 + 1) * P)
+            for i in range(4):
+                nc.tensor.matmul_mx(
+                    out=banks[n % 2][:, i * P : (i + 1) * P],
+                    lhsT=t2_codes[:, i * P : (i + 1) * P].bitcast(FP8X4),
+                    lhsT_scale=t2_plane[:, i * P : (i + 1) * P],
+                    rhs=r_codes[n // 2][:, cols].bitcast(FP8X4),
+                    rhs_scale=r_plane[n // 2][:, cols],
+                    start=True,
+                    stop=True,
+                )
+
+        def turned_scale(n):
+            hi, ap = divmod(TURNED[n], 4)
+            for i in range(4):
+                col = 2 * (4 * (ap - 2) + i) + hi
+                nc.scalar.activation(
+                    out=r_sz[n][:, i * P : (i + 1) * P],
+                    in_=banks[n % 2][:, i * P : (i + 1) * P],
+                    func=COPY,
+                    scale=s_col[:, col : col + 1],
+                )
+
+        def turned_back(n):
+            hi, ap = divmod(TURNED[n], 4)
+            bank = banks[6 + n % 2]
+            nc.tensor.matmul(
+                out=bank[:], lhsT=ident_bf[:], rhs=y_turn[:, hi, (ap - 2) * K : (ap - 1) * K], start=True, stop=False
+            )
+            for i in range(4):
+                nc.tensor.matmul(
+                    out=bank[:, i * P : (i + 1) * P],
+                    lhsT=r_sz[n][:, i * P : (i + 1) * P],
+                    rhs=ident[:],
+                    is_transpose=True,
+                    start=False,
+                    stop=(i == 3),
+                )
+
+        def turned_copy(n):
+            nc.scalar.copy(out=r_res[n][:], in_=banks[6 + n % 2][:])
+
+        def turned_store(n):
+            nc.sync.dma_start(out=o_tok[P : 2 * P, TURNED[n], :], in_=r_res[n][:])
 
         for j in range(4):
             nc.vector.tensor_scalar(
@@ -176,51 +318,109 @@ def tile_quantatwoaxispairtensorupdate_kernel(tc, x, t1, t2_bytes, t2_scale, s, 
             out=t2_codes[:].bitcast(FP8X4), scales=t2_plane[:], in_=t2_grp[:].rearrange("p c j -> p (c j)")
         )
 
-        head_banks = [banks[0], banks[1], banks[6], banks[7]]
+        def finish(pair):
+            u = 2 * pair
+            scale_z(u)
+            scale_z(u + 1)
+            if u + 2 < UNITS:
+                quant_h(u + 2, 2)
+                second_product(u + 2)
+                second_product(u + 3)
+
+        for c in range(4):
+            order_x(c)
         for rr in range(4):
-            turn_x(0, rr, head_banks[rr])
-            copy_x(0, rr, head_banks[rr])
-
-        interleave(t1_grp, t1_raw)
-        nc.vector.quantize_mx(
-            out=t1_codes[:, 1, :].bitcast(FP8X4), scales=t1_plane[:], in_=t1_grp[:].rearrange("p c j -> p (c j)")
-        )
+            turn_x(0, rr, banks[rr])
+            copy_x(0, rr, banks[rr], 0, 1)
+        for rr in range(4):
+            copy_x(0, rr, banks[rr], 1, 2)
+        group_t1(0)
+        quant_t1(0)
+        spread_t1(0, 0)
+        spread_t1_scales(0)
         quant_x(0, 0, 0, 1)
-        for rh in range(2):
-            nc.vector.tensor_copy(
-                out=w_codes[rh][:].bitcast(I32),
-                in_=t1_codes[:, 1 - rh : 3 - rh, :].bitcast(I32).rearrange("p z c -> p c z"),
-            )
-            nc.vector.tensor_copy(out=w_plane[:, :, rh], in_=t1_plane[:])
+        first_pass(0, 0)
+        first_pass(1, 0)
+        spread_t1(0, 1)
         quant_x(0, 1, 0, 1)
-        turn_x(1, 0, t_banks[0])
-
-        first_product(0)
-        first_product(1)
+        first_pass(0, 1)
+        copy_h(0)
+        first_pass(1, 1)
+        copy_h(1)
+        order_late_x(0)
         quant_x(0, 0, 1, 2)
+        order_late_x(1)
+        quant_x(0, 1, 1, 2)
+        turn_x(1, 0, banks[0])
+        turn_x(1, 1, banks[1])
+        copy_x(1, 0, banks[0], 0, 2)
+        first_product(2)
         quant_h(0, 1)
         second_product(0)
-        first_product(2)
-        for step in range(1, UNITS + 1):
-            if step == 1:
-                copy_x(1, 0, t_banks[0])
-                quant_h(1, 1)
-            if step < 4:
-                turn_x(1, step, t_banks[step % 2])
-            if step + LEAD - 1 < UNITS:
-                first_product(step + LEAD - 1)
-            if step % 2 == 0 and step < UNITS:
-                quant_h(step, 2)
-            if step < UNITS:
-                second_product(step)
-            if step == 1:
-                quant_x(0, 1, 1, 2)
-            if step < 4:
-                copy_x(1, step, t_banks[step % 2])
-            scale_z(step - 1)
-            if step in (3, 5):
-                quant_x(1, (step - 3) // 2, 0, 2)
-            if step % 2 == 1 and step >= 3:
-                add_store(step - 3, 2)
-        add_store(UNITS - 2, 1)
-        add_store(UNITS - 1, 1)
+        first_product(3)
+        group_t1(1)
+        quant_h(1, 1)
+        second_product(1)
+        quant_t1(1)
+        scale_z(0)
+        spread_t1(1, 0)
+        spread_t1_scales(1)
+        spread_t1(1, 1)
+        copy_x(1, 1, banks[1], 0, 2)
+        turn_x(1, 2, banks[0])
+        first_product(4)
+        first_product(5)
+        scale_z(1)
+        quant_h(2, 2)
+        second_product(2)
+        second_product(3)
+        turn_x(1, 3, banks[1])
+        copy_x(1, 2, banks[0], 0, 2)
+        copy_x(1, 3, banks[1], 0, 2)
+        first_product(6)
+        first_product(7)
+        add_store(0, 2)
+        quant_x(1, 0, 0, 2)
+        finish(1)
+        turn_s(banks[0])
+        quant_x(1, 1, 0, 2)
+        turned_first(0)
+        turned_first(1)
+        first_product(8)
+        first_product(9)
+        turned_first(2)
+        turned_first(3)
+        add_store(2, 2)
+        finish(2)
+        turned_quant(0)
+        turned_second(0)
+        turned_second(1)
+        turned_scale(0)
+        first_product(10)
+        first_product(11)
+        turned_scale(1)
+        turned_back(0)
+        add_store(4, 2)
+        finish(3)
+        turned_back(1)
+        turned_quant(1)
+        turned_second(2)
+        turned_second(3)
+        turned_copy(0)
+        turned_copy(1)
+        turned_scale(2)
+        turned_store(0)
+        add_store(6, 2)
+        turned_store(1)
+        turned_back(2)
+        finish(4)
+        turned_scale(3)
+        turned_back(3)
+        turned_copy(2)
+        turned_copy(3)
+        turned_store(2)
+        add_store(8, 2)
+        turned_store(3)
+        finish(5)
+        add_store(10, 1)
+        add_store(11, 1)

@@ -19,12 +19,14 @@ COPY = mybir.ActivationFunctionType.Copy
 
 P = 128
 UNITS = 12
-TURNED = (2, 6, 3, 7)
+TURNED_AL = 3
 
 
 def place(u):
-    pair = u // 2
-    return 2 * (pair // 4) + pair % 2, 2 * (pair // 2 % 2) + u % 2
+    tt, v = divmod(u, 6)
+    if v < 4:
+        return 2 * tt + v // 2, v % 2
+    return 2 * tt + v % 2, 2
 
 
 def tile_quantatwoaxispairtensorupdate_kernel(tc, x, t1, t2_bytes, t2_scale, s, y0, out):
@@ -47,11 +49,13 @@ def tile_quantatwoaxispairtensorupdate_kernel(tc, x, t1, t2_bytes, t2_scale, s, 
         banks = [ps.tile([P, 512], F32, name="bank%d" % i) for i in range(8)]
 
         def h_bank(u):
-            return banks[4 + u % 4] if u < 8 else banks[4 + u % 2]
+            return banks[4 + u % 4] if u < 6 else banks[4 + u % 2]
 
         def z_bank(u):
             return banks[2 + u % 2]
 
+        def sum_bank(ah, tt):
+            return banks[6 - 2 * ah + tt]
 
         ident = sb.tile([P, P], F32, align_bytes=256)
         t2_raw = sb.tile([P, 4, K], U8, align_bytes=256)
@@ -67,22 +71,22 @@ def tile_quantatwoaxispairtensorupdate_kernel(tc, x, t1, t2_bytes, t2_scale, s, 
         w_codes = tiles("w_codes", 4, [P, 256, 2], U32)
         w_plane = tiles("w_plane", 2, [P, 256, 2], U8)
         s_sb = sb.tile([P, 4 * K], BF16, align_bytes=256)
-        x_part = tiles("x_part", 4, [P, 1024], BF16)
-        x_late = tiles("x_late", 2, [P, 2048], BF16)
-        x_perm = tiles("x_perm", 2, [P, 16, P], F32)
-        y_sb = tiles("y_sb", 2, [P, 4 * K], BF16) + tiles("y_half", 2, [P, 2 * K], BF16)
-        y_turn = sb.tile([P, 2, 2 * K], BF16, align_bytes=256)
+        x_first = sb.tile([P, 8 * K], BF16, align_bytes=256)
+        x_second = tiles("x_second", 2, [P, 4 * K], BF16)
+        x_sorted = sb.tile([P, 16, P], F32, align_bytes=256)
+        y_sb = tiles("y_sb", 4, [P, 3 * K], BF16)
+        y_turn = tiles("y_turn", 2, [P, 2, K], BF16)
         ident_bf = sb.tile([P, P], BF16, align_bytes=256)
-        s_col = sb.tile([P, 16], F32, align_bytes=256)
-        r_grp = tiles("r_grp", 2, [P, 1024], BF16)
-        r_codes = tiles("r_codes", 2, [P, 2 * P], U32)
-        r_plane = tiles("r_plane", 2, [P, 2 * P], U8)
-        r_sz = tiles("r_sz", 4, [P, K], F32)
-        r_res = tiles("r_res", 4, [P, K], F32)
-        x_grp = tiles("x_grp", 4, [P, 2048], BF16)
-        x_codes = tiles("x_codes", 4, [P, 512], U32)
-        x_plane = tiles("x_plane", 4, [P, 512], U8)
-        h_grp = tiles("h_grp", UNITS // 2, [P, 1024], BF16)
+        s_col = sb.tile([P, 8], F32, align_bytes=256)
+        turn_grp = tiles("turn_grp", 2, [P, 2 * K], BF16)
+        turn_codes = tiles("turn_codes", 2, [P, 2 * P], U32)
+        turn_plane = tiles("turn_plane", 2, [P, 2 * P], U8)
+        turn_sz = tiles("turn_sz", 2, [P, 4, 2 * P], F32)
+        turn_res = tiles("turn_res", 4, [P, K], F32)
+        x_grp = tiles("x_grp", 4, [P, 4 * K], BF16)
+        x_codes = tiles("x_codes", 4, [P, K], U32)
+        x_plane = tiles("x_plane", 4, [P, K], U8)
+        h_grp = tiles("h_grp", UNITS // 2, [P, 2 * K], BF16)
         h_codes = tiles("h_codes", UNITS // 2, [P, 2 * P], U32)
         h_plane = tiles("h_plane", UNITS // 2, [P, 2 * P], U8)
         sz = tiles("sz", UNITS // 2, [P, 2 * K], F32)
@@ -90,51 +94,45 @@ def tile_quantatwoaxispairtensorupdate_kernel(tc, x, t1, t2_bytes, t2_scale, s, 
 
         nc.sync.dma_start(out=t2_raw[:], in_=t2_bytes.rearrange("(p j) n -> p j n", j=4))
         nc.sync.dma_start(out=t2_sc[:], in_=t2_scale.rearrange("(p j) o -> p (j o)", j=4))
-        for c in range(4):
-            nc.sync.dma_start(out=x_part[c][:], in_=x_rows[0:P, c * 1024 : (c + 1) * 1024])
+        nc.sync.dma_start(out=x_first[:], in_=x_rows[0:P, :])
         nc.sync.dma_start(out=t1_raw[:], in_=t1.rearrange("(p j) n -> p j n", j=4))
         for c in range(2):
-            nc.sync.dma_start(out=x_late[c][:], in_=x_rows[P : 2 * P, c * 2048 : (c + 1) * 2048])
+            nc.sync.dma_start(out=x_second[c][:], in_=x_rows[P : 2 * P, c * 4 * K : (c + 1) * 4 * K])
         nc.sync.dma_start(out=s_sb[:], in_=s_rows.partition_broadcast(64))
-        for g in range(4):
-            nc.sync.dma_start(out=y_sb[g][:], in_=y_rows[g * P : (g + 1) * P, 0 : (4 * K if g < 2 else 2 * K)])
-        nc.sync.dma_start(out=y_turn[:], in_=y_tok[P : 2 * P, :, 2 * K : 4 * K])
+        for band in range(4):
+            nc.sync.dma_start(out=y_sb[band][:], in_=y_rows[band * P : (band + 1) * P, 0 : TURNED_AL * K])
+        for tt in range(2):
+            nc.sync.dma_start(out=y_turn[tt][:], in_=y_tok[tt * P : (tt + 1) * P, :, TURNED_AL * K : 4 * K])
 
         make_identity(nc, ident[:])
-        make_identity(nc, ident_bf[:])
+        nc.scalar.copy(out=ident_bf[:], in_=ident[:])
         for half in range(2):
             nc.gpsimd.memset(t1_codes[half][:, 0, :], 0)
             nc.gpsimd.memset(t1_codes[half][:, 2, :], 0)
             nc.gpsimd.memset(t1_plane[half][:].bitcast(U32), 0)
 
-        def interleave(grp, raw):
+        def sort_x(c):
             nc.vector.tensor_copy(
-                out=grp[:].rearrange("p (c i) j -> p c j i", i=4),
-                in_=raw[:].rearrange("p j (c i) -> p c j i", i=4),
-            )
-
-        def order_x(c):
-            nc.scalar.copy(
-                out=x_perm[0][:, :, c * 32 : (c + 1) * 32].rearrange("p (j r) (g l) -> p j g r l", j=4, l=4),
-                in_=x_part[c][:].bitcast(F32).rearrange("p (g l j r) -> p j g r l", l=4, j=4, r=4),
-            )
-
-        def order_late_x(c):
-            nc.vector.tensor_copy(
-                out=x_perm[1][:, :, c * 64 : (c + 1) * 64].rearrange("p (j r) (g l) -> p j g r l", j=4, l=4),
-                in_=x_late[c][:].bitcast(F32).rearrange("p (g l j r) -> p j g r l", l=4, j=4, r=4),
+                out=x_sorted[:, :, c * 64 : (c + 1) * 64].rearrange("p (j r) (g l) -> p j g r l", j=4, l=4),
+                in_=x_second[c][:].bitcast(F32).rearrange("p (g l j r) -> p j g r l", l=4, j=4, r=4),
             )
 
         def turn_x(tt, rr, bank):
             for j in range(4):
-                nc.tensor.transpose(bank[:, j * P : (j + 1) * P], x_perm[tt][:, 4 * j + rr, :], ident[:])
+                w = 4 * j + rr
+                words = x_first[:].bitcast(F32)[:, w : 4 * K : 16] if tt == 0 else x_sorted[:, w, :]
+                nc.tensor.transpose(bank[:, j * P : (j + 1) * P], words, ident[:])
 
-        def copy_x(tt, rr, bank, lo, hi):
+        def copy_x(tt, rr, bank):
             dst = x_grp[2 * tt + rr // 2][:].rearrange("p (t q e j) -> p t q e j", q=2, e=2, j=4)
             nc.scalar.copy(
-                out=dst[:, lo * 64 : hi * 64, rr % 2, :, :],
-                in_=bank[:].bitcast(BF16).rearrange("p (j t e) -> p t e j", j=4, e=2)[:, lo * 64 : hi * 64, :, :],
+                out=dst[:, :, rr % 2, :, :],
+                in_=bank[:].bitcast(BF16).rearrange("p (j t e) -> p t e j", j=4, e=2),
             )
+
+        def quant_x(tt, rh):
+            n = 2 * tt + rh
+            nc.vector.quantize_mx(out=x_codes[n][:].bitcast(FP8X4), scales=x_plane[n][:], in_=x_grp[n][:])
 
         def group_t1(half):
             nc.vector.tensor_copy(
@@ -159,27 +157,24 @@ def tile_quantatwoaxispairtensorupdate_kernel(tc, x, t1, t2_bytes, t2_scale, s, 
             for z in range(2):
                 nc.vector.tensor_copy(out=w_plane[half][:, :, z], in_=t1_plane[half][:])
 
-        def quant_x(tt, rh, lo, hi):
-            n = 2 * tt + rh
-            nc.vector.quantize_mx(
-                out=x_codes[n][:, lo * 256 : hi * 256].bitcast(FP8X4),
-                scales=x_plane[n][:, lo * 256 : hi * 256],
-                in_=x_grp[n][:, lo * 1024 : hi * 1024],
-            )
+        def stationary_t1(ah, al, rh):
+            own = slice((2 * ah + al % 2) * P, (2 * ah + al % 2 + 1) * P)
+            codes = w_codes[2 * (al // 2) + rh][:].rearrange("p c z -> p (c z)")[:, own]
+            return codes.bitcast(FP8X4), w_plane[al // 2][:].rearrange("p c z -> p (c z)")[:, own]
 
         def first_pass(u, rh):
-            g, ap = place(u)
-            cols = slice((g % 2) * 256, (g % 2 + 1) * 256)
-            for hi in range(2):
-                own = slice((2 * hi + ap % 2) * P, (2 * hi + ap % 2 + 1) * P)
+            band, al = place(u)
+            cols = slice((band % 2) * 256, (band % 2 + 1) * 256)
+            for ah in range(2):
+                codes, plane = stationary_t1(ah, al, rh)
                 nc.tensor.matmul_mx(
-                    out=h_bank(u)[:, hi * 256 : (hi + 1) * 256],
-                    lhsT=w_codes[2 * (ap // 2) + rh][:].rearrange("p c z -> p (c z)")[:, own].bitcast(FP8X4),
-                    lhsT_scale=w_plane[ap // 2][:].rearrange("p c z -> p (c z)")[:, own],
-                    rhs=x_codes[2 * (g // 2) + rh][:, cols].bitcast(FP8X4),
-                    rhs_scale=x_plane[2 * (g // 2) + rh][:, cols],
-                    start=(rh == 0 and hi == 0),
-                    stop=(rh == 1 and hi == 1),
+                    out=h_bank(u)[:, ah * 256 : (ah + 1) * 256],
+                    lhsT=codes,
+                    lhsT_scale=plane,
+                    rhs=x_codes[2 * (band // 2) + rh][:, cols].bitcast(FP8X4),
+                    rhs_scale=x_plane[2 * (band // 2) + rh][:, cols],
+                    start=(rh == 0 and ah == 0),
+                    stop=(rh == 1 and ah == 1),
                 )
 
         def copy_h(u):
@@ -214,96 +209,97 @@ def tile_quantatwoaxispairtensorupdate_kernel(tc, x, t1, t2_bytes, t2_scale, s, 
             )
 
         def scale_z(u):
-            ap = place(u)[1]
+            al = place(u)[1]
             nc.vector.tensor_tensor(
                 out=sz[u // 2][:, (u % 2) * K : (u % 2 + 1) * K],
                 in0=z_bank(u)[:],
-                in1=s_sb[:, ap * K : (ap + 1) * K],
+                in1=s_sb[:, al * K : (al + 1) * K],
                 op=MULT,
             )
 
-        def add_store(u, n):
-            g, ap = place(u)
-            own = slice((u % 2) * K, (u % 2 + n) * K)
-            cols = slice(ap * K, (ap + n) * K)
-            nc.vector.tensor_tensor(out=res[u // 2][:, own], in0=sz[u // 2][:, own], in1=y_sb[g][:, cols], op=ADD)
-            nc.sync.dma_start(out=o_rows[g * P : (g + 1) * P, cols], in_=res[u // 2][:, own])
+        def scale_pair(u):
+            scale_z(u)
+            scale_z(u + 1)
+            if u + 2 < UNITS:
+                quant_h(u + 2, 2)
+                second_product(u + 2)
+                second_product(u + 3)
+
+        def add_store(u, lo, hi):
+            band, al = place(u)
+            own = slice((u % 2) * K + lo, (u % 2) * K + hi)
+            cols = slice(al * K + lo, al * K + hi)
+            nc.vector.tensor_tensor(out=res[u // 2][:, own], in0=sz[u // 2][:, own], in1=y_sb[band][:, cols], op=ADD)
+            nc.sync.dma_start(out=o_rows[band * P : (band + 1) * P, cols], in_=res[u // 2][:, own])
 
         def turn_s(bank):
-            for n in range(8):
+            for i in range(4):
                 nc.tensor.matmul(
-                    out=bank[:, 2 * n : 2 * n + 2],
-                    lhsT=s_sb[:, 2 * K + n * P : 2 * K + (n + 1) * P],
+                    out=bank[:, 2 * i : 2 * i + 2],
+                    lhsT=s_sb[:, TURNED_AL * K + i * P : TURNED_AL * K + (i + 1) * P],
                     rhs=ident_bf[:, 0:2],
                     start=True,
                     stop=True,
                 )
-            nc.scalar.copy(out=s_col[:], in_=bank[:, 0:16])
+            nc.scalar.copy(out=s_col[:], in_=bank[:, 0:8])
 
-        def turned_first(n):
-            hi, ap = divmod(TURNED[n], 4)
-            own = slice((2 * hi + ap % 2) * P, (2 * hi + ap % 2 + 1) * P)
-            bank = banks[6 + n % 2]
+        def turned_first(ah, tt):
+            bank = banks[6 + ah]
             for rh in range(2):
+                codes, plane = stationary_t1(ah, TURNED_AL, rh)
                 nc.tensor.matmul_mx(
                     out=bank[:],
-                    lhsT=w_codes[2 + rh][:].rearrange("p c z -> p (c z)")[:, own].bitcast(FP8X4),
-                    lhsT_scale=w_plane[1][:].rearrange("p c z -> p (c z)")[:, own],
-                    rhs=x_codes[2 + rh][:].bitcast(FP8X4),
-                    rhs_scale=x_plane[2 + rh][:],
+                    lhsT=codes,
+                    lhsT_scale=plane,
+                    rhs=x_codes[2 * tt + rh][:].bitcast(FP8X4),
+                    rhs_scale=x_plane[2 * tt + rh][:],
                     start=(rh == 0),
                     stop=(rh == 1),
                 )
-            nc.scalar.copy(out=r_grp[n // 2][:, (n % 2) * K : (n % 2 + 1) * K], in_=bank[:])
+            nc.scalar.copy(out=turn_grp[ah][:, tt * K : (tt + 1) * K], in_=bank[:])
 
-        def turned_quant(m):
-            nc.vector.quantize_mx(out=r_codes[m][:].bitcast(FP8X4), scales=r_plane[m][:], in_=r_grp[m][:])
+        def turned_quant(ah):
+            nc.vector.quantize_mx(out=turn_codes[ah][:].bitcast(FP8X4), scales=turn_plane[ah][:], in_=turn_grp[ah][:])
 
-        def turned_second(n):
-            cols = slice((n % 2) * P, (n % 2 + 1) * P)
-            for i in range(4):
+        def turned_second(ah, b):
+            for i in (2 * b, 2 * b + 1):
                 nc.tensor.matmul_mx(
-                    out=banks[n % 2][:, i * P : (i + 1) * P],
+                    out=banks[b][:, (i % 2) * 256 : (i % 2 + 1) * 256],
                     lhsT=t2_codes[:, i * P : (i + 1) * P].bitcast(FP8X4),
                     lhsT_scale=t2_plane[:, i * P : (i + 1) * P],
-                    rhs=r_codes[n // 2][:, cols].bitcast(FP8X4),
-                    rhs_scale=r_plane[n // 2][:, cols],
+                    rhs=turn_codes[ah][:].bitcast(FP8X4),
+                    rhs_scale=turn_plane[ah][:],
                     start=True,
                     stop=True,
                 )
 
-        def turned_scale(n):
-            hi, ap = divmod(TURNED[n], 4)
+        def turned_scale(ah):
             for i in range(4):
-                col = 2 * (4 * (ap - 2) + i) + hi
                 nc.scalar.activation(
-                    out=r_sz[n][:, i * P : (i + 1) * P],
-                    in_=banks[n % 2][:, i * P : (i + 1) * P],
+                    out=turn_sz[ah][:, i, :],
+                    in_=banks[i // 2][:, (i % 2) * 256 : (i % 2 + 1) * 256],
                     func=COPY,
-                    scale=s_col[:, col : col + 1],
+                    scale=s_col[:, 2 * i + ah : 2 * i + ah + 1],
                 )
 
-        def turned_back(n):
-            hi, ap = divmod(TURNED[n], 4)
-            bank = banks[6 + n % 2]
-            nc.tensor.matmul(
-                out=bank[:], lhsT=ident_bf[:], rhs=y_turn[:, hi, (ap - 2) * K : (ap - 1) * K], start=True, stop=False
-            )
+        def turned_back(ah, tt):
+            bank = sum_bank(ah, tt)
+            nc.tensor.matmul(out=bank[:], lhsT=ident_bf[:], rhs=y_turn[tt][:, ah, :], start=True, stop=False)
             for i in range(4):
                 nc.tensor.matmul(
                     out=bank[:, i * P : (i + 1) * P],
-                    lhsT=r_sz[n][:, i * P : (i + 1) * P],
+                    lhsT=turn_sz[ah][:, i, tt * P : (tt + 1) * P],
                     rhs=ident[:],
                     is_transpose=True,
                     start=False,
                     stop=(i == 3),
                 )
 
-        def turned_copy(n):
-            nc.scalar.copy(out=r_res[n][:], in_=banks[6 + n % 2][:])
+        def turned_copy(ah, tt):
+            nc.scalar.copy(out=turn_res[2 * ah + tt][:], in_=sum_bank(ah, tt)[:])
 
-        def turned_store(n):
-            nc.sync.dma_start(out=o_tok[P : 2 * P, TURNED[n], :], in_=r_res[n][:])
+        def turned_store(ah, tt):
+            nc.sync.dma_start(out=o_tok[tt * P : (tt + 1) * P, 4 * ah + TURNED_AL, :], in_=turn_res[2 * ah + tt][:])
 
         for j in range(4):
             nc.vector.tensor_scalar(
@@ -313,114 +309,108 @@ def tile_quantatwoaxispairtensorupdate_kernel(tc, x, t1, t2_bytes, t2_scale, s, 
                 scalar2=None,
                 op0=MULT,
             )
-        interleave(t2_grp, t2_wide)
+        nc.vector.tensor_copy(
+            out=t2_grp[:].rearrange("p (c i) j -> p c j i", i=4),
+            in_=t2_wide[:].rearrange("p j (c i) -> p c j i", i=4),
+        )
         nc.vector.quantize_mx(
             out=t2_codes[:].bitcast(FP8X4), scales=t2_plane[:], in_=t2_grp[:].rearrange("p c j -> p (c j)")
         )
 
-        def finish(pair):
-            u = 2 * pair
-            scale_z(u)
-            scale_z(u + 1)
-            if u + 2 < UNITS:
-                quant_h(u + 2, 2)
-                second_product(u + 2)
-                second_product(u + 3)
-
-        for c in range(4):
-            order_x(c)
         for rr in range(4):
             turn_x(0, rr, banks[rr])
-            copy_x(0, rr, banks[rr], 0, 1)
-        for rr in range(4):
-            copy_x(0, rr, banks[rr], 1, 2)
+            copy_x(0, rr, banks[rr])
         group_t1(0)
+        group_t1(1)
         quant_t1(0)
+        sort_x(0)
         spread_t1(0, 0)
+        sort_x(1)
+        for rr in range(2):
+            turn_x(1, rr, banks[rr])
+        for rr in range(2):
+            copy_x(1, rr, banks[rr])
         spread_t1_scales(0)
-        quant_x(0, 0, 0, 1)
+
+        quant_x(0, 0)
         first_pass(0, 0)
         first_pass(1, 0)
         spread_t1(0, 1)
-        quant_x(0, 1, 0, 1)
+        quant_t1(1)
+        quant_x(0, 1)
         first_pass(0, 1)
-        copy_h(0)
         first_pass(1, 1)
+        copy_h(0)
         copy_h(1)
-        order_late_x(0)
-        quant_x(0, 0, 1, 2)
-        order_late_x(1)
-        quant_x(0, 1, 1, 2)
-        turn_x(1, 0, banks[0])
-        turn_x(1, 1, banks[1])
-        copy_x(1, 0, banks[0], 0, 2)
         first_product(2)
+        first_product(3)
+        spread_t1_scales(1)
+        spread_t1(1, 0)
+        spread_t1(1, 1)
+
         quant_h(0, 1)
         second_product(0)
-        first_product(3)
-        group_t1(1)
+        turn_x(1, 2, banks[0])
+        copy_x(1, 2, banks[0])
+        quant_x(1, 0)
         quant_h(1, 1)
         second_product(1)
-        quant_t1(1)
-        scale_z(0)
-        spread_t1(1, 0)
-        spread_t1_scales(1)
-        spread_t1(1, 1)
-        copy_x(1, 1, banks[1], 0, 2)
-        turn_x(1, 2, banks[0])
+        turn_x(1, 3, banks[1])
+        copy_x(1, 3, banks[1])
         first_product(4)
         first_product(5)
-        scale_z(1)
-        quant_h(2, 2)
-        second_product(2)
-        second_product(3)
-        turn_x(1, 3, banks[1])
-        copy_x(1, 2, banks[0], 0, 2)
-        copy_x(1, 3, banks[1], 0, 2)
+
+        scale_pair(0)
+        turned_first(0, 0)
+        turned_first(1, 0)
+        turn_s(banks[0])
+        add_store(0, 0, 2 * K)
+        quant_x(1, 1)
         first_product(6)
         first_product(7)
-        add_store(0, 2)
-        quant_x(1, 0, 0, 2)
-        finish(1)
-        turn_s(banks[0])
-        quant_x(1, 1, 0, 2)
-        turned_first(0)
-        turned_first(1)
+        turned_first(0, 1)
+
+        scale_pair(2)
+        turned_first(1, 1)
         first_product(8)
         first_product(9)
-        turned_first(2)
-        turned_first(3)
-        add_store(2, 2)
-        finish(2)
+        add_store(2, 0, 2 * K)
+
+        scale_pair(4)
         turned_quant(0)
-        turned_second(0)
-        turned_second(1)
+        turned_second(0, 0)
+        turned_second(0, 1)
         turned_scale(0)
         first_product(10)
         first_product(11)
-        turned_scale(1)
-        turned_back(0)
-        add_store(4, 2)
-        finish(3)
-        turned_back(1)
+        add_store(4, 0, K)
         turned_quant(1)
-        turned_second(2)
-        turned_second(3)
-        turned_copy(0)
-        turned_copy(1)
-        turned_scale(2)
-        turned_store(0)
-        add_store(6, 2)
-        turned_store(1)
-        turned_back(2)
-        finish(4)
-        turned_scale(3)
-        turned_back(3)
-        turned_copy(2)
-        turned_copy(3)
-        turned_store(2)
-        add_store(8, 2)
-        turned_store(3)
-        finish(5)
-        add_store(10, 1)
-        add_store(11, 1)
+        turned_second(1, 0)
+        turned_back(0, 0)
+        turned_second(1, 1)
+        turned_copy(0, 0)
+        add_store(5, 0, K)
+
+        scale_pair(6)
+        turned_back(0, 1)
+        turned_scale(1)
+        turned_copy(0, 1)
+        add_store(6, 0, K)
+        turned_store(0, 0)
+        add_store(7, 0, K)
+        turned_back(1, 0)
+        turned_copy(1, 0)
+
+        scale_pair(8)
+        turned_back(1, 1)
+        turned_copy(1, 1)
+        turned_store(0, 1)
+        add_store(8, 0, K)
+        add_store(9, 0, K)
+        turned_store(1, 0)
+        turned_store(1, 1)
+
+        scale_pair(10)
+        add_store(10, 0, K)
+        add_store(11, 0, K // 2)
+        add_store(11, K // 2, K)

@@ -19,6 +19,7 @@ COPY = mybir.ActivationFunctionType.Copy
 
 P = 128
 UNITS = 12
+SORTED = 3
 TURNED_AL = 3
 
 
@@ -73,7 +74,7 @@ def tile_quantatwoaxispairtensorupdate_kernel(tc, x, t1, t2_bytes, t2_scale, s, 
         s_sb = sb.tile([P, 4 * K], BF16, align_bytes=256)
         x_first = sb.tile([P, 8 * K], BF16, align_bytes=256)
         x_second = tiles("x_second", 2, [P, 4 * K], BF16)
-        x_sorted = sb.tile([P, 16, P], F32, align_bytes=256)
+        x_sorted = tiles("x_sorted", 2, [P, 16, P], F32)
         y_sb = tiles("y_sb", 4, [P, 3 * K], BF16)
         y_turn = tiles("y_turn", 2, [P, 2, K], BF16)
         ident_bf = sb.tile([P, P], BF16, align_bytes=256)
@@ -94,7 +95,8 @@ def tile_quantatwoaxispairtensorupdate_kernel(tc, x, t1, t2_bytes, t2_scale, s, 
 
         nc.sync.dma_start(out=t2_raw[:], in_=t2_bytes.rearrange("(p j) n -> p j n", j=4))
         nc.sync.dma_start(out=t2_sc[:], in_=t2_scale.rearrange("(p j) o -> p (j o)", j=4))
-        nc.sync.dma_start(out=x_first[:], in_=x_rows[0:P, :])
+        for c in range(4):
+            nc.sync.dma_start(out=x_first[:, c * 2 * K : (c + 1) * 2 * K], in_=x_rows[0:P, c * 2 * K : (c + 1) * 2 * K])
         nc.sync.dma_start(out=t1_raw[:], in_=t1.rearrange("(p j) n -> p j n", j=4))
         for c in range(2):
             nc.sync.dma_start(out=x_second[c][:], in_=x_rows[P : 2 * P, c * 4 * K : (c + 1) * 4 * K])
@@ -111,16 +113,22 @@ def tile_quantatwoaxispairtensorupdate_kernel(tc, x, t1, t2_bytes, t2_scale, s, 
             nc.gpsimd.memset(t1_codes[half][:, 2, :], 0)
             nc.gpsimd.memset(t1_plane[half][:].bitcast(U32), 0)
 
-        def sort_x(c):
+        def sort_first_x(c):
+            dst = x_sorted[0][:, :, c * 32 : (c + 1) * 32].rearrange("p (j r) (g l) -> p j g r l", j=4, l=4)
+            src = x_first[:].bitcast(F32)[:, c * K : (c + 1) * K].rearrange("p (g l j r) -> p j g r l", l=4, j=4, r=4)
+            nc.scalar.copy(out=dst[:, :, :, 0:SORTED, :], in_=src[:, :, :, 0:SORTED, :])
+
+        def sort_second_x(c):
             nc.vector.tensor_copy(
-                out=x_sorted[:, :, c * 64 : (c + 1) * 64].rearrange("p (j r) (g l) -> p j g r l", j=4, l=4),
+                out=x_sorted[1][:, :, c * 64 : (c + 1) * 64].rearrange("p (j r) (g l) -> p j g r l", j=4, l=4),
                 in_=x_second[c][:].bitcast(F32).rearrange("p (g l j r) -> p j g r l", l=4, j=4, r=4),
             )
 
         def turn_x(tt, rr, bank):
             for j in range(4):
                 w = 4 * j + rr
-                words = x_first[:].bitcast(F32)[:, w : 4 * K : 16] if tt == 0 else x_sorted[:, w, :]
+                as_loaded = tt == 0 and rr >= SORTED
+                words = x_first[:].bitcast(F32)[:, w : 4 * K : 16] if as_loaded else x_sorted[tt][:, w, :]
                 nc.tensor.transpose(bank[:, j * P : (j + 1) * P], words, ident[:])
 
         def copy_x(tt, rr, bank):
@@ -317,15 +325,16 @@ def tile_quantatwoaxispairtensorupdate_kernel(tc, x, t1, t2_bytes, t2_scale, s, 
             out=t2_codes[:].bitcast(FP8X4), scales=t2_plane[:], in_=t2_grp[:].rearrange("p c j -> p (c j)")
         )
 
+        for c in range(4):
+            sort_first_x(c)
         for rr in range(4):
             turn_x(0, rr, banks[rr])
             copy_x(0, rr, banks[rr])
         group_t1(0)
-        group_t1(1)
         quant_t1(0)
-        sort_x(0)
+        sort_second_x(0)
         spread_t1(0, 0)
-        sort_x(1)
+        sort_second_x(1)
         for rr in range(2):
             turn_x(1, rr, banks[rr])
         for rr in range(2):
@@ -336,8 +345,9 @@ def tile_quantatwoaxispairtensorupdate_kernel(tc, x, t1, t2_bytes, t2_scale, s, 
         first_pass(0, 0)
         first_pass(1, 0)
         spread_t1(0, 1)
-        quant_t1(1)
+        group_t1(1)
         quant_x(0, 1)
+        quant_t1(1)
         first_pass(0, 1)
         first_pass(1, 1)
         copy_h(0)

from contextlib import ExitStack

import concourse.mybir as mybir
from concourse.masks import make_identity

T, K = 256, 512
FLOPS = 2 * 2 * (T * 8) * K * K

F32 = mybir.dt.float32
BF16 = mybir.dt.bfloat16
I32 = mybir.dt.int32
U32 = mybir.dt.uint32
U8 = mybir.dt.uint8
FP8 = mybir.dt.float8_e4m3fn
FP8X4 = mybir.dt.float8_e4m3fn_x4
MULT = mybir.AluOpType.mult
ADD = mybir.AluOpType.add
COPY = mybir.ActivationFunctionType.Copy

P = 128
UNITS = 12
SORTED = 3
TURNED_AL = 3


def place(u):
    tt, v = divmod(u, 6)
    if v < 4:
        return 2 * tt + v // 2, v % 2
    return 2 * tt + v % 2, 2


def tile_quantatwoaxispairtensorupdate_kernel(tc, x, t1, t2_bytes, t2_scale, s, y0, out):
    nc = tc.nc
    x_rows = x.rearrange("t p q r -> t (p q r)")
    y_rows = y0.rearrange("t (h a) c d -> (t h) (a c d)", h=2)
    o_rows = out.rearrange("t (h a) c d -> (t h) (a c d)", h=2)
    y_tok = y0.rearrange("t (h a) c d -> t h (a c d)", h=2)
    o_tok = out.rearrange("t a c d -> t a (c d)")
    s_rows = s.rearrange("(h a) c d -> h (a c d)", h=2)

    with ExitStack() as ctx:
        sb = ctx.enter_context(tc.tile_pool(name="sb", bufs=1))
        ps = ctx.enter_context(tc.psum_pool(name="ps", bufs=1))
        ctx.enter_context(tc.manual_schedule())

        def tiles(name, n, shape, dtype):
            return [sb.tile(shape, dtype, name="%s%d" % (name, i), align_bytes=256) for i in range(n)]

        banks = [ps.tile([P, 512], F32, name="bank%d" % i) for i in range(8)]

        def h_bank(u):
            return banks[4 + u % 4] if u < 6 else banks[4 + u % 2]

        def z_bank(u):
            return banks[2 + u % 2]

        def sum_bank(ah, tt):
            return banks[6 - 2 * ah + tt]

        ident = sb.tile([P, P], F32, align_bytes=256)
        t2_raw = sb.tile([P, 4, K], U8, align_bytes=256)
        t2_sc = sb.tile([P, 4], F32, align_bytes=256)
        t2_wide = sb.tile([P, 4, K], BF16, align_bytes=256)
        t2_grp = sb.tile([P, K, 4], BF16, align_bytes=256)
        t2_codes = sb.tile([P, K], U32, align_bytes=256)
        t2_plane = sb.tile([P, K], U8, align_bytes=256)
        t1_raw = sb.tile([P, 4, K], BF16, align_bytes=256)
        t1_grp = tiles("t1_grp", 2, [P, 256, 4], BF16)
        t1_codes = tiles("t1_codes", 2, [P, 3, 256], U32)
        t1_plane = tiles("t1_plane", 2, [P, 256], U8)
        w_codes = tiles("w_codes", 4, [P, 256, 2], U32)
        w_plane = tiles("w_plane", 2, [P, 256, 2], U8)
        s_sb = sb.tile([P, 4 * K], BF16, align_bytes=256)
        x_first = sb.tile([P, 8 * K], BF16, align_bytes=256)
        x_second = tiles("x_second", 2, [P, 4 * K], BF16)
        x_sorted = tiles("x_sorted", 2, [P, 16, P], F32)
        y_sb = tiles("y_sb", 4, [P, 3 * K], BF16)
        y_turn = tiles("y_turn", 2, [P, 2, K], BF16)
        ident_bf = sb.tile([P, P], BF16, align_bytes=256)
        s_col = sb.tile([P, 8], F32, align_bytes=256)
        turn_grp = tiles("turn_grp", 2, [P, 2 * K], BF16)
        turn_codes = tiles("turn_codes", 2, [P, 2 * P], U32)
        turn_plane = tiles("turn_plane", 2, [P, 2 * P], U8)
        turn_sz = tiles("turn_sz", 2, [P, 4, 2 * P], F32)
        turn_res = tiles("turn_res", 4, [P, K], F32)
        x_grp = tiles("x_grp", 4, [P, 4 * K], BF16)
        x_codes = tiles("x_codes", 4, [P, K], U32)
        x_plane = tiles("x_plane", 4, [P, K], U8)
        h_grp = tiles("h_grp", UNITS // 2, [P, 2 * K], BF16)
        h_codes = tiles("h_codes", UNITS // 2, [P, 2 * P], U32)
        h_plane = tiles("h_plane", UNITS // 2, [P, 2 * P], U8)
        sz = tiles("sz", UNITS // 2, [P, 2 * K], F32)
        res = tiles("res", UNITS // 2, [P, 2 * K], F32)

        nc.sync.dma_start(out=t2_raw[:], in_=t2_bytes.rearrange("(p j) n -> p j n", j=4))
        nc.sync.dma_start(out=t2_sc[:], in_=t2_scale.rearrange("(p j) o -> p (j o)", j=4))
        for c in range(4):
            nc.sync.dma_start(out=x_first[:, c * 2 * K : (c + 1) * 2 * K], in_=x_rows[0:P, c * 2 * K : (c + 1) * 2 * K])
        nc.sync.dma_start(out=t1_raw[:], in_=t1.rearrange("(p j) n -> p j n", j=4))
        for c in range(2):
            nc.sync.dma_start(out=x_second[c][:], in_=x_rows[P : 2 * P, c * 4 * K : (c + 1) * 4 * K])
        nc.sync.dma_start(out=s_sb[:], in_=s_rows.partition_broadcast(64))
        for band in range(4):
            nc.sync.dma_start(out=y_sb[band][:], in_=y_rows[band * P : (band + 1) * P, 0 : TURNED_AL * K])
        for tt in range(2):
            nc.sync.dma_start(out=y_turn[tt][:], in_=y_tok[tt * P : (tt + 1) * P, :, TURNED_AL * K : 4 * K])

        make_identity(nc, ident[:])
        nc.scalar.copy(out=ident_bf[:], in_=ident[:])
        for half in range(2):
            nc.gpsimd.memset(t1_codes[half][:, 0, :], 0)
            nc.gpsimd.memset(t1_codes[half][:, 2, :], 0)
            nc.gpsimd.memset(t1_plane[half][:].bitcast(U32), 0)

        def sort_first_x(c):
            dst = x_sorted[0][:, :, c * 32 : (c + 1) * 32].rearrange("p (j r) (g l) -> p j g r l", j=4, l=4)
            src = x_first[:].bitcast(F32)[:, c * K : (c + 1) * K].rearrange("p (g l j r) -> p j g r l", l=4, j=4, r=4)
            nc.scalar.copy(out=dst[:, :, :, 0:SORTED, :], in_=src[:, :, :, 0:SORTED, :])

        def sort_second_x(c):
            nc.vector.tensor_copy(
                out=x_sorted[1][:, :, c * 64 : (c + 1) * 64].rearrange("p (j r) (g l) -> p j g r l", j=4, l=4),
                in_=x_second[c][:].bitcast(F32).rearrange("p (g l j r) -> p j g r l", l=4, j=4, r=4),
            )

        def turn_x(tt, rr, bank):
            for j in range(4):
                w = 4 * j + rr
                as_loaded = tt == 0 and rr >= SORTED
                words = x_first[:].bitcast(F32)[:, w : 4 * K : 16] if as_loaded else x_sorted[tt][:, w, :]
                nc.tensor.transpose(bank[:, j * P : (j + 1) * P], words, ident[:])

        def copy_x(tt, rr, bank):
            dst = x_grp[2 * tt + rr // 2][:].rearrange("p (t q e j) -> p t q e j", q=2, e=2, j=4)
            nc.scalar.copy(
                out=dst[:, :, rr % 2, :, :],
                in_=bank[:].bitcast(BF16).rearrange("p (j t e) -> p t e j", j=4, e=2),
            )

        def quant_x(tt, rh):
            n = 2 * tt + rh
            nc.vector.quantize_mx(out=x_codes[n][:].bitcast(FP8X4), scales=x_plane[n][:], in_=x_grp[n][:])

        def group_t1(half):
            nc.vector.tensor_copy(
                out=t1_grp[half][:].rearrange("p (h c i) j -> p h c j i", h=2, i=4),
                in_=t1_raw[:].rearrange("p j (h f c i) -> p f h c j i", h=2, f=2, i=4)[:, half],
            )

        def quant_t1(half):
            nc.vector.quantize_mx(
                out=t1_codes[half][:, 1, :].bitcast(FP8X4),
                scales=t1_plane[half][:],
                in_=t1_grp[half][:].rearrange("p c j -> p (c j)"),
            )

        def spread_t1(half, rh):
            nc.vector.tensor_copy(
                out=w_codes[2 * half + rh][:].bitcast(I32),
                in_=t1_codes[half][:, 1 - rh : 3 - rh, :].bitcast(I32).rearrange("p z c -> p c z"),
            )

        def spread_t1_scales(half):
            for z in range(2):
                nc.vector.tensor_copy(out=w_plane[half][:, :, z], in_=t1_plane[half][:])

        def stationary_t1(ah, al, rh):
            own = slice((2 * ah + al % 2) * P, (2 * ah + al % 2 + 1) * P)
            codes = w_codes[2 * (al // 2) + rh][:].rearrange("p c z -> p (c z)")[:, own]
            return codes.bitcast(FP8X4), w_plane[al // 2][:].rearrange("p c z -> p (c z)")[:, own]

        def first_pass(u, rh):
            band, al = place(u)
            cols = slice((band % 2) * 256, (band % 2 + 1) * 256)
            for ah in range(2):
                codes, plane = stationary_t1(ah, al, rh)
                nc.tensor.matmul_mx(
                    out=h_bank(u)[:, ah * 256 : (ah + 1) * 256],
                    lhsT=codes,
                    lhsT_scale=plane,
                    rhs=x_codes[2 * (band // 2) + rh][:, cols].bitcast(FP8X4),
                    rhs_scale=x_plane[2 * (band // 2) + rh][:, cols],
                    start=(rh == 0 and ah == 0),
                    stop=(rh == 1 and ah == 1),
                )

        def copy_h(u):
            nc.scalar.copy(
                out=h_grp[u // 2][:, (u % 2) * K : (u % 2 + 1) * K].rearrange("p (t h r) -> p t h r", h=2, r=4),
                in_=h_bank(u)[:].rearrange("p (h t r) -> p t h r", h=2, r=4),
            )

        def first_product(u):
            first_pass(u, 0)
            first_pass(u, 1)
            copy_h(u)

        def quant_h(u, n):
            lo, hi = u % 2, u % 2 + n
            nc.vector.quantize_mx(
                out=h_codes[u // 2][:, lo * P : hi * P].bitcast(FP8X4),
                scales=h_plane[u // 2][:, lo * P : hi * P],
                in_=h_grp[u // 2][:, lo * K : hi * K],
            )

        def second_product(u):
            cols = slice((u % 2) * P, (u % 2 + 1) * P)
            nc.tensor.matmul_mx(
                out=z_bank(u)[:],
                lhsT=h_codes[u // 2][:, cols].bitcast(FP8X4),
                lhsT_scale=h_plane[u // 2][:, cols],
                rhs=t2_codes[:].bitcast(FP8X4),
                rhs_scale=t2_plane[:],
                start=True,
                stop=True,
            )

        def scale_z(u):
            al = place(u)[1]
            nc.vector.tensor_tensor(
                out=sz[u // 2][:, (u % 2) * K : (u % 2 + 1) * K],
                in0=z_bank(u)[:],
                in1=s_sb[:, al * K : (al + 1) * K],
                op=MULT,
            )

        def scale_pair(u):
            scale_z(u)
            scale_z(u + 1)
            if u + 2 < UNITS:
                quant_h(u + 2, 2)
                second_product(u + 2)
                second_product(u + 3)

        def add_store(u, lo, hi):
            band, al = place(u)
            own = slice((u % 2) * K + lo, (u % 2) * K + hi)
            cols = slice(al * K + lo, al * K + hi)
            nc.vector.tensor_tensor(out=res[u // 2][:, own], in0=sz[u // 2][:, own], in1=y_sb[band][:, cols], op=ADD)
            nc.sync.dma_start(out=o_rows[band * P : (band + 1) * P, cols], in_=res[u // 2][:, own])

        def turn_s(bank):
            for i in range(4):
                nc.tensor.matmul(
                    out=bank[:, 2 * i : 2 * i + 2],
                    lhsT=s_sb[:, TURNED_AL * K + i * P : TURNED_AL * K + (i + 1) * P],
                    rhs=ident_bf[:, 0:2],
                    start=True,
                    stop=True,
                )
            nc.scalar.copy(out=s_col[:], in_=bank[:, 0:8])

        def turned_first(ah, tt):
            bank = banks[6 + ah]
            for rh in range(2):
                codes, plane = stationary_t1(ah, TURNED_AL, rh)
                nc.tensor.matmul_mx(
                    out=bank[:],
                    lhsT=codes,
                    lhsT_scale=plane,
                    rhs=x_codes[2 * tt + rh][:].bitcast(FP8X4),
                    rhs_scale=x_plane[2 * tt + rh][:],
                    start=(rh == 0),
                    stop=(rh == 1),
                )
            nc.scalar.copy(out=turn_grp[ah][:, tt * K : (tt + 1) * K], in_=bank[:])

        def turned_quant(ah):
            nc.vector.quantize_mx(out=turn_codes[ah][:].bitcast(FP8X4), scales=turn_plane[ah][:], in_=turn_grp[ah][:])

        def turned_second(ah, b):
            for i in (2 * b, 2 * b + 1):
                nc.tensor.matmul_mx(
                    out=banks[b][:, (i % 2) * 256 : (i % 2 + 1) * 256],
                    lhsT=t2_codes[:, i * P : (i + 1) * P].bitcast(FP8X4),
                    lhsT_scale=t2_plane[:, i * P : (i + 1) * P],
                    rhs=turn_codes[ah][:].bitcast(FP8X4),
                    rhs_scale=turn_plane[ah][:],
                    start=True,
                    stop=True,
                )

        def turned_scale(ah):
            for i in range(4):
                nc.scalar.activation(
                    out=turn_sz[ah][:, i, :],
                    in_=banks[i // 2][:, (i % 2) * 256 : (i % 2 + 1) * 256],
                    func=COPY,
                    scale=s_col[:, 2 * i + ah : 2 * i + ah + 1],
                )

        def turned_back(ah, tt):
            bank = sum_bank(ah, tt)
            nc.tensor.matmul(out=bank[:], lhsT=ident_bf[:], rhs=y_turn[tt][:, ah, :], start=True, stop=False)
            for i in range(4):
                nc.tensor.matmul(
                    out=bank[:, i * P : (i + 1) * P],
                    lhsT=turn_sz[ah][:, i, tt * P : (tt + 1) * P],
                    rhs=ident[:],
                    is_transpose=True,
                    start=False,
                    stop=(i == 3),
                )

        def turned_copy(ah, tt):
            nc.scalar.copy(out=turn_res[2 * ah + tt][:], in_=sum_bank(ah, tt)[:])

        def turned_store(ah, tt):
            nc.sync.dma_start(out=o_tok[tt * P : (tt + 1) * P, 4 * ah + TURNED_AL, :], in_=turn_res[2 * ah + tt][:])

        for j in range(4):
            nc.vector.tensor_scalar(
                out=t2_wide[:, j, :],
                in0=t2_raw[:, j, :].bitcast(FP8),
                scalar1=t2_sc[:, j : j + 1],
                scalar2=None,
                op0=MULT,
            )
        nc.vector.tensor_copy(
            out=t2_grp[:].rearrange("p (c i) j -> p c j i", i=4),
            in_=t2_wide[:].rearrange("p j (c i) -> p c j i", i=4),
        )
        nc.vector.quantize_mx(
            out=t2_codes[:].bitcast(FP8X4), scales=t2_plane[:], in_=t2_grp[:].rearrange("p c j -> p (c j)")
        )

        for c in range(4):
            sort_first_x(c)
        for rr in range(4):
            turn_x(0, rr, banks[rr])
            copy_x(0, rr, banks[rr])
        group_t1(0)
        quant_t1(0)
        sort_second_x(0)
        spread_t1(0, 0)
        sort_second_x(1)
        for rr in range(2):
            turn_x(1, rr, banks[rr])
        for rr in range(2):
            copy_x(1, rr, banks[rr])
        spread_t1_scales(0)

        quant_x(0, 0)
        first_pass(0, 0)
        first_pass(1, 0)
        spread_t1(0, 1)
        group_t1(1)
        quant_x(0, 1)
        quant_t1(1)
        first_pass(0, 1)
        first_pass(1, 1)
        copy_h(0)
        copy_h(1)
        first_product(2)
        first_product(3)
        spread_t1_scales(1)
        spread_t1(1, 0)
        spread_t1(1, 1)

        quant_h(0, 1)
        second_product(0)
        turn_x(1, 2, banks[0])
        copy_x(1, 2, banks[0])
        quant_x(1, 0)
        quant_h(1, 1)
        second_product(1)
        turn_x(1, 3, banks[1])
        copy_x(1, 3, banks[1])
        first_product(4)
        first_product(5)

        scale_pair(0)
        turned_first(0, 0)
        turned_first(1, 0)
        turn_s(banks[0])
        add_store(0, 0, 2 * K)
        quant_x(1, 1)
        first_product(6)
        first_product(7)
        turned_first(0, 1)

        scale_pair(2)
        turned_first(1, 1)
        first_product(8)
        first_product(9)
        add_store(2, 0, 2 * K)

        scale_pair(4)
        turned_quant(0)
        turned_second(0, 0)
        turned_second(0, 1)
        turned_scale(0)
        first_product(10)
        first_product(11)
        add_store(4, 0, K)
        turned_quant(1)
        turned_second(1, 0)
        turned_back(0, 0)
        turned_second(1, 1)
        turned_copy(0, 0)
        add_store(5, 0, K)

        scale_pair(6)
        turned_back(0, 1)
        turned_scale(1)
        turned_copy(0, 1)
        add_store(6, 0, K)
        turned_store(0, 0)
        add_store(7, 0, K)
        turned_back(1, 0)
        turned_copy(1, 0)

        scale_pair(8)
        turned_back(1, 1)
        turned_copy(1, 1)
        turned_store(0, 1)
        add_store(8, 0, K)
        add_store(9, 0, K)
        turned_store(1, 0)
        turned_store(1, 1)

        scale_pair(10)
        add_store(10, 0, K)
        add_store(11, 0, K // 2)
        add_store(11, K // 2, K)
